import numpy as np
import ml_dtypes


def mxq(x, axis, fmt="e4m3"):
    dtype, down = {"e4m3": (ml_dtypes.float8_e4m3fn, 7), "e5m2": (ml_dtypes.float8_e5m2, 14)}[fmt]
    v = np.moveaxis(np.asarray(x, np.float32).astype(ml_dtypes.bfloat16).astype(np.float64), axis, -1)
    blocks = v.reshape(v.shape[:-1] + (-1, 32))
    amax = np.abs(blocks).max(-1, keepdims=True)
    byte = np.maximum(np.where(amax > 0, np.frexp(amax)[1] - 1 + 127, 0) - down, 1)
    scale = np.exp2(byte - 127.0)
    codes = (blocks / scale).astype(np.float32).astype(dtype).astype(np.float64)
    return np.moveaxis((codes * scale).reshape(v.shape), -1, axis)


WIDE = False


def mx_kscale(k):
    if not WIDE:
        return np.ones(k)
    levels = np.array([10, -10, 5, -5, 0])
    if k % 512:
        return np.exp2(np.random.permutation(np.resize(levels, k // 32))).repeat(32)
    a = np.empty((k // 512, 16))
    for p in range(k // 512):
        a[p, :8] = np.random.permutation(np.resize(levels, 8))
        for g in range(8):
            far = levels[np.abs(levels - a[p, g]) >= 10]
            a[p, g + 8] = far[np.random.randint(len(far))]
    return np.exp2(a.ravel()).repeat(32)


def f64(x):
    return np.asarray(x).astype(np.float64)


def striped(idx):
    return np.tile(idx.reshape(-1, 16).T, (8, 1)).astype(np.uint16)


def unstriped(offs):
    return offs[:16].T.reshape(-1).astype(np.int64)


E2M1 = np.array([0.0, 0.5, 1.0, 1.5, 2.0, 3.0, 4.0, 6.0, -0.0, -0.5, -1.0, -1.5, -2.0, -3.0, -4.0, -6.0])


def pack_weight(w, fmt):
    k, n = w.shape
    w = f64(np.asarray(w, np.float32).astype(ml_dtypes.bfloat16)).reshape(k // 32, 32, n)
    amax = np.abs(w).max(1)
    if fmt == "e4m3":
        byte = np.frexp(amax)[1] - 1 + 127 - 7
    else:
        mant, ex = np.frexp(amax / 6.0)
        byte = np.where(mant > 0.5, ex, ex - 1) + 127
    byte = np.clip(np.where(amax > 0, byte, 1), 1, 254)
    scaled = (w * np.exp2(127.0 - byte)[:, None, :]).reshape(k, n).astype(np.float32)
    by_word = np.ascontiguousarray(scaled.reshape(k // 512, 128, 4, n).transpose(0, 1, 3, 2))
    if fmt == "e4m3":
        words = by_word.astype(ml_dtypes.float8_e4m3fn).view(np.uint8)
    else:
        c = by_word.astype(ml_dtypes.float4_e2m1fn).view(np.uint8) & 0xF
        words = (c[..., 0::2] | (c[..., 1::2] << 4)).reshape(k // 512, 128, 2 * n)
    return np.ascontiguousarray(words), np.ascontiguousarray(byte.astype(np.uint8).reshape(k // 512, 16, n))


def unpack_weight(words, scales, fmt):
    g, _, n = scales.shape
    words = np.ascontiguousarray(words).reshape(g, 128, n, -1)
    if fmt == "e4m3":
        vals = words.view(ml_dtypes.float8_e4m3fn).astype(np.float64)
    else:
        nib = np.empty((g, 128, n, 4), np.uint8)
        nib[..., 0::2] = words & 0xF
        nib[..., 1::2] = words >> 4
        vals = E2M1[nib]
    vals = vals * np.repeat(np.exp2(scales.astype(np.float64) - 127.0), 8, axis=1)[..., None]
    return vals.transpose(0, 1, 3, 2).reshape(g * 512, n)


def gelu(v):
    return 0.5 * v * (1.0 + np.tanh(np.sqrt(2.0 / np.pi) * (v + 0.044715 * v**3)))


def striped8(idx):
    return np.concatenate([v.reshape(-1, 16).T for v in idx]).astype(np.uint16)


def unstriped8(offs):
    return np.stack([offs[16 * g:16 * g + 16].T.reshape(-1) for g in range(8)]).astype(np.int64)


def heads(h, wgt, idx8):
    r = np.arange(h.shape[0])
    return wgt[r // 4 % 128] * h[r[:, None], idx8[r % 512 // 64]]


def put_heads(h, wgs, idx8, t2):
    r = np.arange(h.shape[0])
    page = np.zeros((h.shape[0], t2))
    page[r[:, None], idx8[r % 512 // 64]] = wgs[r // 4 % 128] * h
    return page


K, T, S, P, T2, H, N = 1024, 4096, 1024, 512, 1024, 512, 1024

def setup_inputs():
    n = np.random.standard_normal
    s = mx_kscale(K)[:, None]
    u = mx_kscale(H)[:, None]
    d = {}
    d["tab_words"], d["tab_scales"] = pack_weight(n((K, T)) * s, "e4m3")
    d["offs"] = striped(np.random.permutation(T)[:S])
    d["w1"] = (n((K, H)) / s * u.T / K ** 0.5).astype(np.float32)
    d["w2_words"], d["w2_scales"] = pack_weight(n((K, H)) / s * u.T / K ** 0.5, "e4m3")
    d["w3"] = (0.8 * n((H, H)) / u / H ** 0.5).astype(np.float32)
    d["base"] = (0.7 * np.exp(0.3 * n(H)) / u[:, 0]).astype(np.float32)
    d["wgt"] = np.repeat(np.random.uniform(0.5, 2.0, (8, P)), 16, axis=0).astype(np.float32)
    d["offs2"] = striped8(np.stack([np.random.permutation(S)[:P] for _ in range(8)]))
    d["bias"] = (0.6 * n(H)).astype(np.float32)
    d["gain"] = (np.exp(0.3 * n(H)) * u[:, 0]).astype(np.float32)
    d["w4_words"], d["w4_scales"] = pack_weight(n((H, N)) / u / H ** 0.5, "e2m1")
    d["climate"] = np.exp(0.5 * n((N, P))).astype(np.float32)
    d["wgo"] = np.repeat(np.random.uniform(0.5, 2.0, (8, P)), 16, axis=0).astype(np.float32)
    d["offs3"] = striped8(np.stack([np.random.permutation(T2)[:P] for _ in range(8)]))
    return d

def reference(tab_words, tab_scales, offs, w1, w2_words, w2_scales, w3, base, wgt, offs2, bias, gain, w4_words, w4_scales, climate, wgo, offs3):
    v = unpack_weight(tab_words, tab_scales, "e4m3")[:, unstriped(offs)]
    a = mxq(f64(w1), 0, "e4m3").T @ v
    b = unpack_weight(w2_words, w2_scales, "e4m3").T @ v
    top = np.maximum(a, b)
    h = mxq(f64(w3), 0, "e4m3").T @ mxq(top, 0, "e4m3")
    h = h - f64(base)[:, None] * a
    x = heads(h, f64(wgt), unstriped8(offs2))
    z = np.tanh(x + f64(bias)[:, None]) * f64(gain)[:, None]
    y = unpack_weight(w4_words, w4_scales, "e2m1").T @ mxq(z, 0, "e4m3")
    y = y * f64(climate)
    return put_heads(y, f64(wgo), unstriped8(offs3), T2)

from contextlib import ExitStack

import concourse.mybir as mybir

K, T, S, M, T2, H, N = 1024, 4096, 1024, 512, 1024, 512, 1024
FLOPS = 2 * (2 * K * H * S + H * H * S + H * N * M)

F32 = mybir.dt.float32
BF16 = mybir.dt.bfloat16
I32 = mybir.dt.int32
U32 = mybir.dt.uint32
U16 = mybir.dt.uint16
U8 = mybir.dt.uint8
E4M3 = mybir.dt.float8_e4m3fn_x4
E2M1 = mybir.dt.float4_e2m1fn_x4
ALU = mybir.AluOpType
ACT = mybir.ActivationFunctionType

P = 128
BANK = 512
PRE_ON_GPSIMD = True
SPLIT_TILES = 4
EARLY_TILES = 3


def tile_list_humidification_need_slots_kernel(
    tc, tab_words, tab_scales, offs, w1, w2_words, w2_scales, w3, base, wgt, offs2,
    bias, gain, w4_words, w4_scales, climate, wgo, offs3, out,
):
    nc = tc.nc
    with ExitStack() as ctx:
        lists = ctx.enter_context(tc.tile_pool(name="lists", bufs=1))
        sb = ctx.enter_context(tc.tile_pool(name="sb", bufs=1))
        psum = ctx.enter_context(tc.psum_pool(name="psum", bufs=1))

        def tile(name, shape, dtype, tag=None):
            return sb.tile(shape, dtype, name=name, tag=tag or name, align_bytes=64)

        def bank(k, name, shape):
            return psum.tile(shape, F32, name=name, tag="bank%d" % k)

        idx1 = lists.tile([P, S // 16], U16, name="idx1")
        idx2 = lists.tile([P, M // 16], U16, name="idx2")
        idx3 = lists.tile([P, M // 16], U16, name="idx3")

        tab = [tile("tab%d" % a, [P, T], U32) for a in range(2)]
        tab_sc = tile("tab_sc", [P, T], U8)
        w2_raw = tile("w2_raw", [P, 2, H], U32)
        w2_sc_raw = tile("w2_sc_raw", [P, H], U8)
        w4_raw = tile("w4_raw", [P, N], U16)
        w4_sc_raw = tile("w4_sc_raw", [P, N], U8)
        w1_raw = [tile("w1_raw%d" % a, [P, 4, H], F32, tag="w1_then_a%d" % a) for a in range(2)]
        w3_raw = tile("w3_raw", [P, 4, H], F32)
        base_sb = tile("base_sb", [P, 4], F32)
        bias_sb = tile("bias_sb", [P, 4], F32)
        gain_sb = tile("gain_sb", [P, 4], F32)
        wgt_sb = tile("wgt_sb", [P, M], F32)
        wgo_sb = tile("wgo_sb", [P, M], F32)
        clim = [tile("clim%d" % q, [P, 2, M], F32) for q in range(4)]
        pages = [tile("page%d" % t, [P, T2], F32) for t in range(8)]

        nc.vector.memset(tab_sc[:].bitcast(I32), 0)
        for plane in (w2_sc_raw, w4_sc_raw):
            nc.gpsimd.memset(plane[:].bitcast(I32), 0)

        def load_scales(queue, plane, scales):
            rows = 4 * scales.shape[0]
            for q in range(4):
                queue.dma_start(
                    out=plane[32 * q : 32 * q + rows, :].bitcast(I32),
                    in_=scales[:, 4 * q : 4 * q + 4, :].bitcast(I32),
                )

        def load_words(dst, words):
            nc.sync.dma_start(out=dst, in_=words.bitcast(I32))

        def load_table(a, q):
            quarter = slice(q * T // 4, (q + 1) * T // 4)
            load_words(tab[a][:, quarter].bitcast(I32), tab_words[a, :, quarter, :].rearrange("p t i -> p (t i)"))

        nc.sync.dma_start(idx1[:], offs)
        for q in range(2):
            load_table(0, q)
        nc.sync.dma_start(idx2[:], offs2)
        nc.sync.dma_start(idx3[:], offs3)
        for dst, vec in ((base_sb, base), (bias_sb, bias), (gain_sb, gain)):
            nc.sync.dma_start(out=dst[:], in_=vec.rearrange("(p i) -> p i", i=4))
        for q in range(2, 4):
            load_table(0, q)
        for a in range(2):
            load_words(w2_raw[:, a, :].bitcast(I32), w2_words[a].rearrange("p c i -> p (c i)"))
        load_scales(nc.sync, tab_sc, tab_scales)
        load_table(1, 0)
        load_scales(nc.sync, w2_sc_raw, w2_scales)
        for q in range(1, 4):
            load_table(1, q)
        for a in range(2):
            nc.sync.dma_start(out=w1_raw[a][:], in_=w1[512 * a : 512 * (a + 1), :].rearrange("(p j) c -> p j c", j=4))
        nc.sync.dma_start(out=w3_raw[:], in_=w3.rearrange("(p j) c -> p j c", j=4))
        nc.sync.dma_start(out=wgo_sb[:], in_=wgo)
        clim_rows = climate.rearrange("(b p i) m -> p b i m", b=2, i=4)
        for q in range(4):
            nc.sync.dma_start(out=clim[q][:], in_=clim_rows[:, q // 2, 2 * (q % 2) : 2 * (q % 2) + 2, :])
        nc.sync.dma_start(out=wgt_sb[:], in_=wgt)
        load_words(w4_raw[:].bitcast(I32), w4_words[0])
        load_scales(nc.sync, w4_sc_raw, w4_scales)

        for n_tile, page in enumerate(pages):
            (nc.vector if n_tile < 5 else nc.gpsimd).memset(page[:], 0.0)

        w2_sc = tile("w2_sc", [P, H], U8)
        nc.vector.tensor_copy(out=w2_sc[:].rearrange("p (t m) -> p t m", t=4), in_=w2_sc_raw[:].rearrange("p (m t) -> p t m", t=4))
        w2_codes = tile("w2_codes", [P, 2, H], U32)
        nc.scalar.copy(
            out=w2_codes[:].rearrange("p a (t m) -> p a t m", t=4), in_=w2_raw[:].rearrange("p a (m t) -> p a t m", t=4)
        )

        v_codes = [[tile("v%d_%d" % (a, hf), [P, BANK], U32) for hf in range(2)] for a in range(2)]
        v_sc = [tile("v_sc%d" % hf, [P, BANK], U8) for hf in range(2)]

        def half_list(idx, hf):
            cols = idx.shape[1] // 2
            return idx[:, hf * cols : (hf + 1) * cols]

        for hf in range(2):
            nc.vector.tensor_copy(out=v_codes[0][hf][:], in_=tab[0][:].indirect(half_list(idx1, hf)))
            nc.vector.tensor_copy(out=v_sc[hf][:], in_=tab_sc[:].indirect(half_list(idx1, hf)))
        for hf in range(2):
            nc.vector.tensor_copy(out=v_codes[1][hf][:], in_=tab[1][:].indirect(half_list(idx1, hf)))

        def mx(out_ap, lhs, lhs_sc, rhs, rhs_sc, start, stop, lhs_fmt=E4M3):
            nc.tensor.matmul_mx(
                out=out_ap, lhsT=lhs.bitcast(lhs_fmt), lhsT_scale=lhs_sc, rhs=rhs.bitcast(E4M3), rhs_scale=rhs_sc,
                start=start, stop=stop,
            )

        def slot(t):
            return slice(P * t, P * (t + 1))

        b_ps = [bank(k, "b_ps%d" % k, [P, BANK]) for k in range(8)]
        b_sb = [tile("b_sb%d" % hf, [P, 4, BANK], F32) for hf in range(2)]
        for a in range(2):
            for k in range(8):
                hf, t = divmod(k, 4)
                mx(b_ps[k][:], w2_codes[:, a, slot(t)], w2_sc[4 * a :, slot(t)], v_codes[a][hf][:], v_sc[hf][4 * a :, :], a == 0, a == 1)
                if a == 1:
                    nc.scalar.copy(out=b_sb[hf][:, t, :], in_=b_ps[k][:])

        def round_weight(copy, name, raw, tag):
            dealt = tile(name + "_bf", [P, 4 * H], BF16, tag=tag)
            copy(
                out=dealt[:].rearrange("p (u e m j) -> p u m j e", u=2, e=2, j=4),
                in_=raw[:].rearrange("p j (m u e) -> p u m j e", u=2, e=2),
            )
            return dealt

        def quantise(name, values):
            width = values.shape[1] // 4
            codes = tile(name + "_codes", [P, width], U32)
            scales = tile(name + "_sc", [P, width], U8)
            nc.vector.quantize_mx(out=codes[:].bitcast(E4M3), scales=scales[:], in_=values)
            return codes, scales

        w1_q = []
        for a in range(2):
            w1_bf = round_weight(nc.vector.tensor_copy, "w1_%d" % a, w1_raw[a], "w1_bf%d" % a)
            w1_q.append(quantise("w1_%d" % a, w1_bf[:]))

        a_ps = [bank(c, "a_ps%d" % c, [P, 4, P]) for c in range(8)]
        for a in range(2):
            for c in range(8):
                hf, cc = divmod(c, 4)
                for t in range(4):
                    mx(a_ps[c][:, t, :], w1_q[a][0][:, slot(t)], w1_q[a][1][:, slot(t)], v_codes[a][hf][:, slot(cc)],
                       v_sc[hf][4 * a :, slot(cc)], a == 0 and t == 0, a == 1 and t == 3)

        w3_bf = round_weight(nc.scalar.copy, "w3", w3_raw, "w1_bf0")
        neg_base = tile("neg_base", [P, 4], F32)
        nc.vector.tensor_scalar(out=neg_base[:], in0=base_sb[:], scalar1=-1.0, scalar2=None, op0=ALU.mult)

        def woven(ap):
            return ap.rearrange("p (c e t) -> p c t e", e=2, t=4)

        def planar(ap):
            return ap.rearrange("p t (c e) -> p c t e", e=2)

        a_sb = [tile("a_sb%d" % hf, [P, 4, BANK], F32, tag="w1_then_a%d" % hf) for hf in range(2)]
        top = [tile("top%d" % hf, [P, 4 * BANK], BF16) for hf in range(2)]
        h = [tile("h%d" % t, [P, S], F32) for t in range(4)]
        top_q = []

        def maxima(c):
            hf, cc = divmod(c, 4)
            nc.vector.tensor_tensor(
                out=woven(top[hf][:, BANK * cc : BANK * (cc + 1)]), in0=planar(a_ps[c][:]), in1=planar(b_sb[hf][:, :, slot(cc)]), op=ALU.max
            )
            nc.scalar.copy(out=a_sb[hf][:, :, slot(cc)], in_=a_ps[c][:])

        def second_stage(hf, t):
            h_ps = bank(4 * hf + t, "h_ps%d_%d" % (hf, t), [P, BANK])
            mx(h_ps[:], w3_q[0][:, slot(t)], w3_q[1][:, slot(t)], top_q[hf][0][:], top_q[hf][1][:], True, True)
            nc.vector.scalar_tensor_tensor(
                out=h[t][:, BANK * hf : BANK * (hf + 1)], in0=a_sb[hf][:, t, :], scalar=neg_base[:, t : t + 1], in1=h_ps[:],
                op0=ALU.mult, op1=ALU.add,
            )

        for c in range(5):
            maxima(c)
        top_q.append(quantise("top0", top[0][:]))
        maxima(5)
        w3_q = quantise("w3", w3_bf[:])
        maxima(6)
        maxima(7)
        second_stage(0, 0)
        top_q.append(quantise("top1", top[1][:]))
        for t in range(1, 4):
            second_stage(0, t)
        for t in range(4):
            second_stage(1, t)

        def clim_of(n_tile):
            return clim[n_tile // 2][:, n_tile % 2, :]

        if PRE_ON_GPSIMD:
            for n_tile in range(8):
                nc.gpsimd.tensor_tensor(out=clim_of(n_tile), in0=clim_of(n_tile), in1=wgo_sb[:], op=ALU.mult)

        w4_codes = tile("w4_codes", [P, N], U16)
        nc.scalar.copy(
            out=w4_codes[:].rearrange("p (b t m) -> p b t m", b=2, t=4), in_=w4_raw[:].rearrange("p (b m t) -> p b t m", b=2, t=4)
        )
        w4_sc = tile("w4_sc", [P, N], U8)
        nc.gpsimd.tensor_copy(
            out=w4_sc[:].rearrange("p (b t m) -> p b t m", b=2, t=4), in_=w4_sc_raw[:].rearrange("p (b m t) -> p b t m", b=2, t=4)
        )

        HALF = M // 2
        z_codes = tile("z_codes", [P, M], U32)
        z_sc = tile("z_sc", [P, M], U8)
        x = [tile("x%d" % hf, [P, 4, HALF], F32) for hf in range(2)]

        def cols(hf):
            return slice(HALF * hf, HALF * (hf + 1))

        def pick(hf):
            for t in range(4):
                nc.vector.tensor_tensor(out=x[hf][:, t, :], in0=h[t][:].indirect(half_list(idx2, hf)), in1=wgt_sb[:, cols(hf)], op=ALU.mult)

        def activate(hf):
            for t in range(4):
                nc.scalar.activation(out=x[hf][:, t, :], in_=x[hf][:, t, :], func=ACT.Tanh, bias=bias_sb[:, t : t + 1])
                nc.scalar.activation(out=x[hf][:, t, :], in_=x[hf][:, t, :], func=ACT.Copy, scale=gain_sb[:, t : t + 1])
            z_bf = tile("z_bf%d" % hf, [P, 4 * HALF], BF16)
            nc.scalar.copy(out=woven(z_bf[:]), in_=planar(x[hf][:]))
            nc.vector.quantize_mx(out=z_codes[:, cols(hf)].bitcast(E4M3), scales=z_sc[:, cols(hf)], in_=z_bf[:])

        out_rows = out.rearrange("(b p i) s -> p b i s", b=2, i=4)
        y_ps = [bank(n_tile, "y_ps%d" % n_tile, [P, M]) for n_tile in range(8)]

        def product(n_tile, m_cols, name):
            width = m_cols.stop - m_cols.start
            mx(y_ps[n_tile][:, m_cols], w4_codes[:, slot(n_tile)], w4_sc[:, slot(n_tile)], z_codes[:, m_cols], z_sc[:, m_cols], True, True, E2M1)
            y = tile(name, [P, width], F32)
            if PRE_ON_GPSIMD:
                nc.scalar.copy(out=y[:], in_=y_ps[n_tile][:, m_cols])
            else:
                nc.vector.tensor_tensor(out=y[:], in0=y_ps[n_tile][:, m_cols], in1=clim_of(n_tile)[:, m_cols], op=ALU.mult)
            return y

        def place(n_tile, m_cols, offsets, name):
            y = product(n_tile, m_cols, name)
            factor = clim_of(n_tile)[:, m_cols] if PRE_ON_GPSIMD else wgo_sb[:, m_cols]
            nc.vector.tensor_tensor(out=pages[n_tile][:].indirect(offsets), in0=y[:], in1=factor, op=ALU.mult)

        def store(n_tile):
            nc.sync.dma_start(out=out_rows[:, n_tile // 4, n_tile % 4, :], in_=pages[n_tile][:])

        pick(0)
        pick(1)
        activate(0)
        for n_tile in range(EARLY_TILES):
            place(n_tile, cols(0), half_list(idx3, 0), "y0_%d" % n_tile)
        activate(1)
        for n_tile in range(EARLY_TILES, SPLIT_TILES):
            place(n_tile, cols(0), half_list(idx3, 0), "y0_%d" % n_tile)
        for n_tile in range(SPLIT_TILES):
            place(n_tile, cols(1), half_list(idx3, 1), "y1_%d" % n_tile)
            store(n_tile)
        for n_tile in range(SPLIT_TILES, 8):
            place(n_tile, slice(0, M), idx3[:], "y_%d" % n_tile)
            store(n_tile)
